import numpy as np
import ml_dtypes


def mxq(x, axis, fmt="e4m3"):
    dtype, down = {"e4m3": (ml_dtypes.float8_e4m3fn, 7), "e5m2": (ml_dtypes.float8_e5m2, 14)}[fmt]
    v = np.moveaxis(np.asarray(x, np.float32).astype(ml_dtypes.bfloat16).astype(np.float64), axis, -1)
    blocks = v.reshape(v.shape[:-1] + (-1, 32))
    amax = np.abs(blocks).max(-1, keepdims=True)
    byte = np.maximum(np.where(amax > 0, np.frexp(amax)[1] - 1 + 127, 0) - down, 1)
    scale = np.exp2(byte - 127.0)
    codes = (blocks / scale).astype(np.float32).astype(dtype).astype(np.float64)
    return np.moveaxis((codes * scale).reshape(v.shape), -1, axis)


WIDE = False


def mx_kscale(k):
    if not WIDE:
        return np.ones(k)
    levels = np.array([10, -10, 5, -5, 0])
    if k % 512:
        return np.exp2(np.random.permutation(np.resize(levels, k // 32))).repeat(32)
    a = np.empty((k // 512, 16))
    for p in range(k // 512):
        a[p, :8] = np.random.permutation(np.resize(levels, 8))
        for g in range(8):
            far = levels[np.abs(levels - a[p, g]) >= 10]
            a[p, g + 8] = far[np.random.randint(len(far))]
    return np.exp2(a.ravel()).repeat(32)


def f64(x):
    return np.asarray(x).astype(np.float64)


def striped(idx):
    return np.tile(idx.reshape(-1, 16).T, (8, 1)).astype(np.uint16)


def unstriped(offs):
    return offs[:16].T.reshape(-1).astype(np.int64)


def relu(v):
    return np.maximum(v, 0.0)


K, T, D, S, V, H, N = 1024, 1024, 4, 512, 256, 1024, 256


def setup_inputs():
    n = np.random.standard_normal
    s = mx_kscale(K)[:, None]
    u = mx_kscale(H)
    return {
        "xT": (n((K, T)) * s).astype(np.float32),
        "w1": (n((K, H)) / np.sqrt(K) / s * u).astype(np.float32),
        "w2": (n((H, N)) / np.sqrt(H) / u[:, None]).astype(np.float32),
        "gate": np.tile(np.random.uniform(0.2, 1.0, (D, 1, V)) / np.sqrt(D), (1, N, 1)).astype(np.float32),
        "offs": striped(np.random.permutation(T)[:S]),
        "pos1": striped(np.random.permutation(S)[:V]),
        "pos2": striped(np.random.permutation(S)[:V]),
        "pos3": striped(np.random.permutation(S)[:V]),
        "pos4": striped(np.random.permutation(S)[:V]),
    }


def reference(xT, w1, w2, gate, offs, pos1, pos2, pos3, pos4):
    idx = unstriped(offs)
    xq = mxq(f64(xT)[:, idx], 0, "e4m3")
    h = relu(mxq(f64(w1), 0, "e4m3").T @ xq)
    y = mxq(f64(w2), 0, "e4m3").T @ mxq(h, 0, "e4m3")
    return sum(f64(gate[d]) * y[:, unstriped(p)] for d, p in enumerate((pos1, pos2, pos3, pos4)))

@@ -1,0 +1,211 @@
+from contextlib import ExitStack
+
+import concourse.mybir as mybir
+
+K, T, D, S, V, H, N = 1024, 1024, 4, 512, 256, 1024, 256
+FLOPS = 2 * S * (K * H + H * N) + 2 * D * N * V
+
+F32 = mybir.dt.float32
+BF16 = mybir.dt.bfloat16
+U32 = mybir.dt.uint32
+U16 = mybir.dt.uint16
+U8 = mybir.dt.uint8
+FP8X4 = mybir.dt.float8_e4m3fn_x4
+MULT = mybir.AluOpType.mult
+COPY = mybir.ActivationFunctionType.Copy
+RELU = mybir.ActivationFunctionType.Relu
+
+P = 128
+PACK = 4
+PASS = P * PACK
+X_COLS = 512
+QUARTER = 128
+HALF = 256
+
+
+def tile_picked_sub_mlp_relu_sub_e_kernel(tc, xT, w1, w2, gate, offs, pos1, pos2, pos3, pos4, out):
+    nc = tc.nc
+    passes = K // PASS
+    halves = H // PASS
+
+    with ExitStack() as ctx:
+        lists = ctx.enter_context(tc.tile_pool(name="lists", bufs=1))
+        keep = ctx.enter_context(tc.tile_pool(name="keep", bufs=1))
+        psum_h = ctx.enter_context(tc.psum_pool(name="psum_h", bufs=6))
+        psum_y = ctx.enter_context(tc.psum_pool(name="psum_y", bufs=1))
+
+        x_scales = keep.tile([P, T], U8, align_bytes=64, name="x_scales")
+        nc.gpsimd.memset(x_scales[:], 0)
+        warm = keep.tile([P, 1], F32, name="warm")
+        nc.vector.memset(warm[:], 0.0)
+        warm_out = keep.tile([P, 1], F32, name="warm_out")
+        nc.scalar.activation(out=warm_out[:], in_=warm[:], func=RELU)
+
+        x_raw = {}
+        for s in range(passes):
+            for c in range(T // X_COLS):
+                x_raw[s, c] = keep.tile([P, PACK, X_COLS], F32, name=f"x_raw_{s}_{c}")
+                view = xT[s * PASS : (s + 1) * PASS, c * X_COLS : (c + 1) * X_COLS].rearrange("(p j) w -> p j w", j=PACK)
+                if s == 0 and c == 0:
+                    for a in (0, HALF):
+                        nc.sync.dma_start(out=x_raw[s, c][:, :, a : a + HALF], in_=view[:, :, a : a + HALF])
+                else:
+                    nc.sync.dma_start(out=x_raw[s, c][:], in_=view)
+        offs_t = lists.tile([P, S // 16], U16, name="offs_t")
+        nc.sync.dma_start(offs_t[:], offs)
+        w1_raw = {}
+        pos_t = []
+        for h in range(halves):
+            for s in range(passes):
+                w1_raw[h, s] = keep.tile([P, PACK, PASS], F32, name=f"w1_raw_{h}_{s}")
+                view = w1[s * PASS : (s + 1) * PASS, h * PASS : (h + 1) * PASS].rearrange("(p j) w -> p j w", j=PACK)
+                if h == halves - 1 and s == passes - 1:
+                    for a in (0, HALF):
+                        nc.sync.dma_start(out=w1_raw[h, s][:, :, a : a + HALF], in_=view[:, :, a : a + HALF])
+                else:
+                    nc.sync.dma_start(out=w1_raw[h, s][:], in_=view)
+        w2_raw = {}
+        for s in range(halves):
+            w2_raw[s] = keep.tile([P, PACK, N], F32, name=f"w2_raw_{s}")
+            nc.sync.dma_start(out=w2_raw[s][:], in_=w2[s * PASS : (s + 1) * PASS, :].rearrange("(p j) w -> p j w", j=PACK))
+        for d, pos in enumerate((pos1, pos2, pos3, pos4)):
+            p_t = lists.tile([P, V // 16], U16, name=f"pos_{d}")
+            nc.sync.dma_start(p_t[:], pos)
+            pos_t.append(p_t)
+        gate_t = []
+        for m in range(N // P):
+            g_t = keep.tile([P, D, V], F32, name=f"gate_{m}")
+            nc.sync.dma_start(out=g_t[:], in_=gate[:, m * P : (m + 1) * P, :].rearrange("d p v -> p d v"))
+            gate_t.append(g_t)
+
+        x_words = [keep.tile([P, T], U32, align_bytes=64, name=f"x_words_{s}") for s in range(passes)]
+        xg_words = [keep.tile([P, S], U32, align_bytes=64, name=f"xg_words_{s}") for s in range(passes)]
+        xg_scales = keep.tile([P, S], U8, align_bytes=64, name="xg_scales")
+        w1_words, w1_scales, h_words, h_scales, w2_words, w2_scales = {}, {}, {}, {}, {}, {}
+
+        def cast(eng, out, in_):
+            if eng == "v":
+                nc.vector.tensor_copy(out=out, in_=in_)
+            else:
+                nc.scalar.activation(out=out, in_=in_, func=COPY)
+
+        def x_stage(s, c, parts):
+            grp = keep.tile([P, X_COLS, PACK], BF16, align_bytes=64, name=f"x_grp_{s}_{c}")
+            for a, b, eng in parts:
+                dst = grp[:, a:b, :].rearrange("p (c i) j -> p c j i", i=4)
+                src = x_raw[s, c][:, :, a:b].rearrange("p j (c i) -> p c j i", i=4)
+                cast(eng, dst, src)
+            nc.vector.quantize_mx(
+                out=x_words[s][:, c * X_COLS : (c + 1) * X_COLS].bitcast(FP8X4),
+                scales=x_scales[4 * s : P, c * X_COLS : (c + 1) * X_COLS],
+                in_=grp[:].rearrange("p c j -> p (c j)"),
+            )
+
+        def x_gather(s):
+            nc.vector.tensor_copy(out=xg_words[s][:], in_=x_words[s][:].indirect(offs_t[:]))
+
+        def x_gather_scales():
+            nc.vector.tensor_copy(out=xg_scales[:], in_=x_scales[:].indirect(offs_t[:]))
+
+        def w1_stage(h, s, parts, t_quant):
+            grp = keep.tile([P, PACK, P, PACK], BF16, align_bytes=64, name=f"w1_grp_{h}_{s}")
+            for a, b, eng in parts:
+                dst = grp[:, :, a:b, :].rearrange("p t m j -> p m t j")
+                src = w1_raw[h, s][:, :, PACK * a : PACK * b].rearrange("p j (m t) -> p m t j", t=PACK)
+                cast(eng, dst, src)
+            w1_words[h, s] = keep.tile([P, PASS], U32, align_bytes=64, name=f"w1_words_{h}_{s}")
+            w1_scales[h, s] = keep.tile([P, PASS], U8, align_bytes=64, name=f"w1_scales_{h}_{s}")
+            for t in range(0, PACK, t_quant):
+                cols = slice(t * P, (t + t_quant) * P)
+                nc.vector.quantize_mx(
+                    out=w1_words[h, s][:, cols].bitcast(FP8X4),
+                    scales=w1_scales[h, s][:, cols],
+                    in_=grp[:, t : t + t_quant, :, :].rearrange("p t m j -> p (t m j)"),
+                )
+
+        def h_stage(h, engines, q_quant):
+            h_words[h] = keep.tile([P, S], U32, align_bytes=64, name=f"h_words_{h}")
+            h_scales[h] = keep.tile([P, S], U8, align_bytes=64, name=f"h_scales_{h}")
+            hg = keep.tile([P, S, PACK], BF16, align_bytes=64, name=f"h_grp_{h}")
+            for q in range(S // QUARTER):
+                cols = slice(q * QUARTER, (q + 1) * QUARTER)
+                bank = psum_h.tile([P, PACK, QUARTER], F32, name="h_bank")
+                for t in range(PACK):
+                    for s in range(passes):
+                        nc.tensor.matmul_mx(
+                            out=bank[:, t, :],
+                            lhsT=w1_words[h, s][:, t * P : (t + 1) * P].bitcast(FP8X4),
+                            lhsT_scale=w1_scales[h, s][:, t * P : (t + 1) * P],
+                            rhs=xg_words[s][:, cols].bitcast(FP8X4),
+                            rhs_scale=xg_scales[4 * s : P, cols],
+                            start=(s == 0),
+                            stop=(s == passes - 1),
+                        )
+                src = bank[:].rearrange("p t n -> p n t")
+                if engines[q] == "v":
+                    nc.vector.tensor_scalar_max(out=hg[:, cols, :], in0=src, scalar1=0.0)
+                else:
+                    nc.scalar.activation(out=hg[:, cols, :], in_=src, func=RELU)
+                if (q + 1) % q_quant == 0:
+                    cols = slice((q + 1 - q_quant) * QUARTER, (q + 1) * QUARTER)
+                    nc.vector.quantize_mx(
+                        out=h_words[h][:, cols].bitcast(FP8X4),
+                        scales=h_scales[h][:, cols],
+                        in_=hg[:, cols, :].rearrange("p n t -> p (n t)"),
+                    )
+
+        def w2_stage(s, parts):
+            grp = keep.tile([P, N, PACK], BF16, align_bytes=64, name=f"w2_grp_{s}")
+            for a, b, eng in parts:
+                dst = grp[:, a:b, :].rearrange("p (c i) j -> p c j i", i=4)
+                src = w2_raw[s][:, :, a:b].rearrange("p j (c i) -> p c j i", i=4)
+                cast(eng, dst, src)
+            w2_words[s] = keep.tile([P, N], U32, align_bytes=64, name=f"w2_words_{s}")
+            w2_scales[s] = keep.tile([P, N], U8, align_bytes=64, name=f"w2_scales_{s}")
+            nc.vector.quantize_mx(
+                out=w2_words[s][:].bitcast(FP8X4), scales=w2_scales[s][:], in_=grp[:].rearrange("p c j -> p (c j)")
+            )
+
+        x_stage(0, 0, ((0, 256, "v"), (256, 512, "s"),))
+        x_stage(0, 1, ((0, 256, "v"), (256, 512, "s"),))
+        x_stage(1, 0, ((0, 256, "v"), (256, 512, "s"),))
+        x_stage(1, 1, ((0, 256, "v"), (256, 512, "s"),))
+        x_gather(0)
+        x_gather(1)
+        x_gather_scales()
+        w1_stage(0, 0, ((0, 48, "v"), (48, 128, "s"),), 4)
+        w1_stage(0, 1, ((0, 48, "v"), (48, 128, "s"),), 4)
+        w1_stage(1, 0, ((0, 48, "v"), (48, 128, "s"),), 4)
+        w1_stage(1, 1, ((0, 48, "v"), (48, 64, "s"), (64, 112, "v"), (112, 128, "s"),), 4)
+        h_stage(0, "ssss", 2)
+        w2_stage(0, ((0, 256, "v"),))
+        w2_stage(1, ((0, 128, "v"), (128, 256, "s"),))
+        h_stage(1, "ssvs", 1)
+
+        y_bank = [psum_y.tile([P, S], F32, name=f"y_bank_{m}") for m in range(N // P)]
+        y = [keep.tile([P, S], F32, name=f"y_{m}") for m in range(N // P)]
+        for n0 in range(0, S, HALF):
+            cols = slice(n0, n0 + HALF)
+            for m in range(N // P):
+                m_cols = slice(m * P, (m + 1) * P)
+                for s in range(halves):
+                    nc.tensor.matmul_mx(
+                        out=y_bank[m][:, cols],
+                        lhsT=w2_words[s][:, m_cols].bitcast(FP8X4),
+                        lhsT_scale=w2_scales[s][:, m_cols],
+                        rhs=h_words[s][:, cols].bitcast(FP8X4),
+                        rhs_scale=h_scales[s][:, cols],
+                        start=(s == 0),
+                        stop=(s == halves - 1),
+                    )
+                nc.scalar.activation(out=y[m][:, cols], in_=y_bank[m][:, cols], func=COPY)
+
+        for m in range(N // P):
+            prod = keep.tile([P, D, V], F32, name=f"prod_{m}")
+            for d in range(D):
+                nc.vector.tensor_tensor(prod[:, d, :], y[m][:].indirect(pos_t[d][:]), gate_t[m][:, d, :], MULT)
+            pair = keep.tile([P, 2, V], F32, name=f"pair_{m}")
+            nc.vector.tensor_add(pair[:], prod[:, 0:2, :], prod[:, 2:4, :])
+            total = keep.tile([P, V], F32, name=f"total_{m}")
+            nc.vector.tensor_add(total[:], pair[:, 0, :], pair[:, 1, :])
+            nc.sync.dma_start(out=out[m * P : (m + 1) * P, :], in_=total[:])

@@ -20,7 +20,6 @@ PACK = 4
 PASS = P * PACK
 X_COLS = 512
 QUARTER = 128
-HALF = 256
 
 
 def tile_picked_sub_mlp_relu_sub_e_kernel(tc, xT, w1, w2, gate, offs, pos1, pos2, pos3, pos4, out):
@@ -41,42 +40,34 @@ def tile_picked_sub_mlp_relu_sub_e_kernel(tc, xT, w1, w2, gate, offs, pos1, pos2
         warm_out = keep.tile([P, 1], F32, name="warm_out")
         nc.scalar.activation(out=warm_out[:], in_=warm[:], func=RELU)
 
-        x_raw = {}
+        x_raw = []
         for s in range(passes):
-            for c in range(T // X_COLS):
-                x_raw[s, c] = keep.tile([P, PACK, X_COLS], F32, name=f"x_raw_{s}_{c}")
-                view = xT[s * PASS : (s + 1) * PASS, c * X_COLS : (c + 1) * X_COLS].rearrange("(p j) w -> p j w", j=PACK)
-                if s == 0 and c == 0:
-                    for a in (0, HALF):
-                        nc.sync.dma_start(out=x_raw[s, c][:, :, a : a + HALF], in_=view[:, :, a : a + HALF])
-                else:
-                    nc.sync.dma_start(out=x_raw[s, c][:], in_=view)
+            x_raw.append(keep.tile([P, PACK, T], F32, name=f"x_raw_{s}"))
+            nc.sync.dma_start(
+                out=x_raw[s][:].rearrange("p j w -> p (j w)"),
+                in_=xT[s * PASS : (s + 1) * PASS, :].rearrange("(p j) w -> p (j w)", j=PACK),
+            )
         offs_t = lists.tile([P, S // 16], U16, name="offs_t")
         nc.sync.dma_start(offs_t[:], offs)
         w1_raw = {}
-        pos_t = []
         for h in range(halves):
             for s in range(passes):
                 w1_raw[h, s] = keep.tile([P, PACK, PASS], F32, name=f"w1_raw_{h}_{s}")
                 view = w1[s * PASS : (s + 1) * PASS, h * PASS : (h + 1) * PASS].rearrange("(p j) w -> p j w", j=PACK)
-                if h == halves - 1 and s == passes - 1:
-                    for a in (0, HALF):
-                        nc.sync.dma_start(out=w1_raw[h, s][:, :, a : a + HALF], in_=view[:, :, a : a + HALF])
-                else:
-                    nc.sync.dma_start(out=w1_raw[h, s][:], in_=view)
+                nc.sync.dma_start(out=w1_raw[h, s][:], in_=view)
         w2_raw = {}
         for s in range(halves):
             w2_raw[s] = keep.tile([P, PACK, N], F32, name=f"w2_raw_{s}")
-            nc.sync.dma_start(out=w2_raw[s][:], in_=w2[s * PASS : (s + 1) * PASS, :].rearrange("(p j) w -> p j w", j=PACK))
-        for d, pos in enumerate((pos1, pos2, pos3, pos4)):
-            p_t = lists.tile([P, V // 16], U16, name=f"pos_{d}")
+            nc.sync.dma_start(
+                out=w2_raw[s][:].rearrange("p j w -> p (j w)"),
+                in_=w2[s * PASS : (s + 1) * PASS, :].rearrange("(p j) w -> p (j w)", j=PACK),
+            )
+        gate_t = [keep.tile([P, D, V], F32, name=f"gate_{m}") for m in range(N // P)]
+        pos_t = [lists.tile([P, V // 16], U16, name=f"pos_{d}") for d in range(D)]
+        nc.sync.dma_start(out=gate_t[0][:], in_=gate[:, 0:P, :].rearrange("d p v -> p d v"))
+        for p_t, pos in zip(pos_t, (pos1, pos2, pos3, pos4)):
             nc.sync.dma_start(p_t[:], pos)
-            pos_t.append(p_t)
-        gate_t = []
-        for m in range(N // P):
-            g_t = keep.tile([P, D, V], F32, name=f"gate_{m}")
-            nc.sync.dma_start(out=g_t[:], in_=gate[:, m * P : (m + 1) * P, :].rearrange("d p v -> p d v"))
-            gate_t.append(g_t)
+        nc.sync.dma_start(out=gate_t[1][:], in_=gate[:, P : 2 * P, :].rearrange("d p v -> p d v"))
 
         x_words = [keep.tile([P, T], U32, align_bytes=64, name=f"x_words_{s}") for s in range(passes)]
         xg_words = [keep.tile([P, S], U32, align_bytes=64, name=f"xg_words_{s}") for s in range(passes)]
@@ -93,7 +84,7 @@ def tile_picked_sub_mlp_relu_sub_e_kernel(tc, xT, w1, w2, gate, offs, pos1, pos2
             grp = keep.tile([P, X_COLS, PACK], BF16, align_bytes=64, name=f"x_grp_{s}_{c}")
             for a, b, eng in parts:
                 dst = grp[:, a:b, :].rearrange("p (c i) j -> p c j i", i=4)
-                src = x_raw[s, c][:, :, a:b].rearrange("p j (c i) -> p c j i", i=4)
+                src = x_raw[s][:, :, c * X_COLS + a : c * X_COLS + b].rearrange("p j (c i) -> p c j i", i=4)
                 cast(eng, dst, src)
             nc.vector.quantize_mx(
                 out=x_words[s][:, c * X_COLS : (c + 1) * X_COLS].bitcast(FP8X4),
@@ -166,26 +157,26 @@ def tile_picked_sub_mlp_relu_sub_e_kernel(tc, xT, w1, w2, gate, offs, pos1, pos2
                 out=w2_words[s][:].bitcast(FP8X4), scales=w2_scales[s][:], in_=grp[:].rearrange("p c j -> p (c j)")
             )
 
-        x_stage(0, 0, ((0, 256, "v"), (256, 512, "s"),))
-        x_stage(0, 1, ((0, 256, "v"), (256, 512, "s"),))
+        x_stage(0, 0, ((0, 192, "v"), (192, 512, "s"),))
+        x_stage(0, 1, ((0, 320, "v"), (320, 512, "s"),))
         x_stage(1, 0, ((0, 256, "v"), (256, 512, "s"),))
-        x_stage(1, 1, ((0, 256, "v"), (256, 512, "s"),))
+        x_stage(1, 1, ((0, 192, "v"), (192, 512, "s"),))
         x_gather(0)
         x_gather(1)
         x_gather_scales()
-        w1_stage(0, 0, ((0, 48, "v"), (48, 128, "s"),), 4)
-        w1_stage(0, 1, ((0, 48, "v"), (48, 128, "s"),), 4)
-        w1_stage(1, 0, ((0, 48, "v"), (48, 128, "s"),), 4)
-        w1_stage(1, 1, ((0, 48, "v"), (48, 64, "s"), (64, 112, "v"), (112, 128, "s"),), 4)
+        w1_stage(0, 0, ((0, 40, "v"), (40, 128, "s"),), 4)
+        w1_stage(0, 1, ((0, 40, "v"), (40, 128, "s"),), 4)
+        w1_stage(1, 0, ((0, 40, "v"), (40, 128, "s"),), 4)
+        w1_stage(1, 1, ((0, 80, "v"), (80, 128, "s"),), 4)
         h_stage(0, "ssss", 2)
-        w2_stage(0, ((0, 256, "v"),))
+        w2_stage(0, ((0, 128, "v"), (128, 256, "s"),))
         w2_stage(1, ((0, 128, "v"), (128, 256, "s"),))
-        h_stage(1, "ssvs", 1)
+        h_stage(1, "svss", 1)
 
         y_bank = [psum_y.tile([P, S], F32, name=f"y_bank_{m}") for m in range(N // P)]
         y = [keep.tile([P, S], F32, name=f"y_{m}") for m in range(N // P)]
-        for n0 in range(0, S, HALF):
-            cols = slice(n0, n0 + HALF)
+        for n0, n1 in ((0, 256), (256, 384), (384, 512)):
+            cols = slice(n0, n1)
             for m in range(N // P):
                 m_cols = slice(m * P, (m + 1) * P)
                 for s in range(halves):

@@ -18,7 +18,6 @@ RELU = mybir.ActivationFunctionType.Relu
 P = 128
 PACK = 4
 PASS = P * PACK
-X_COLS = 512
 QUARTER = 128
 
 
@@ -30,31 +29,40 @@ def tile_picked_sub_mlp_relu_sub_e_kernel(tc, xT, w1, w2, gate, offs, pos1, pos2
     with ExitStack() as ctx:
         lists = ctx.enter_context(tc.tile_pool(name="lists", bufs=1))
         keep = ctx.enter_context(tc.tile_pool(name="keep", bufs=1))
-        psum_h = ctx.enter_context(tc.psum_pool(name="psum_h", bufs=6))
-        psum_y = ctx.enter_context(tc.psum_pool(name="psum_y", bufs=1))
+        psum = ctx.enter_context(tc.psum_pool(name="psum", bufs=1))
 
-        x_scales = keep.tile([P, T], U8, align_bytes=64, name="x_scales")
-        nc.gpsimd.memset(x_scales[:], 0)
         warm = keep.tile([P, 1], F32, name="warm")
         nc.vector.memset(warm[:], 0.0)
         warm_out = keep.tile([P, 1], F32, name="warm_out")
         nc.scalar.activation(out=warm_out[:], in_=warm[:], func=RELU)
 
-        x_raw = []
-        for s in range(passes):
-            x_raw.append(keep.tile([P, PACK, T], F32, name=f"x_raw_{s}"))
-            nc.sync.dma_start(
-                out=x_raw[s][:].rearrange("p j w -> p (j w)"),
-                in_=xT[s * PASS : (s + 1) * PASS, :].rearrange("(p j) w -> p (j w)", j=PACK),
-            )
         offs_t = lists.tile([P, S // 16], U16, name="offs_t")
         nc.sync.dma_start(offs_t[:], offs)
-        w1_raw = {}
-        for h in range(halves):
-            for s in range(passes):
-                w1_raw[h, s] = keep.tile([P, PACK, PASS], F32, name=f"w1_raw_{h}_{s}")
-                view = w1[s * PASS : (s + 1) * PASS, h * PASS : (h + 1) * PASS].rearrange("(p j) w -> p j w", j=PACK)
-                nc.sync.dma_start(out=w1_raw[h, s][:], in_=view)
+        x_raw, w1_raw = {}, {}
+
+        def load_x(s, j):
+            x_raw[s, j] = keep.tile([P, T], F32, name=f"x_raw_{s}_{j}")
+            view = xT[s * PASS : (s + 1) * PASS, :].rearrange("(p j) w -> p j w", j=PACK)
+            nc.sync.dma_start(out=x_raw[s, j][:], in_=view[:, j, :])
+
+        def load_w1(h, s, cuts):
+            w1_raw[h, s] = keep.tile([P, PACK, PASS], F32, name=f"w1_raw_{h}_{s}")
+            view = w1[s * PASS : (s + 1) * PASS, h * PASS : (h + 1) * PASS].rearrange("(p j) w -> p j w", j=PACK)
+            for a, b in zip(cuts[:-1], cuts[1:]):
+                nc.sync.dma_start(out=w1_raw[h, s][:, :, a:b], in_=view[:, :, a:b])
+
+        load_x(0, 0)
+        load_x(0, 1)
+        load_x(0, 2)
+        load_x(0, 3)
+        load_x(1, 0)
+        load_x(1, 1)
+        load_x(1, 2)
+        load_w1(0, 0, (0, PASS))
+        load_x(1, 3)
+        load_w1(0, 1, (0, PASS))
+        load_w1(1, 0, (0, PASS))
+        load_w1(1, 1, (0, PASS // 2, PASS))
         w2_raw = {}
         for s in range(halves):
             w2_raw[s] = keep.tile([P, PACK, N], F32, name=f"w2_raw_{s}")
@@ -69,9 +77,9 @@ def tile_picked_sub_mlp_relu_sub_e_kernel(tc, xT, w1, w2, gate, offs, pos1, pos2
             nc.sync.dma_start(p_t[:], pos)
         nc.sync.dma_start(out=gate_t[1][:], in_=gate[:, P : 2 * P, :].rearrange("d p v -> p d v"))
 
-        x_words = [keep.tile([P, T], U32, align_bytes=64, name=f"x_words_{s}") for s in range(passes)]
-        xg_words = [keep.tile([P, S], U32, align_bytes=64, name=f"xg_words_{s}") for s in range(passes)]
-        xg_scales = keep.tile([P, S], U8, align_bytes=64, name="xg_scales")
+        x_words = [keep.tile([P, S], U32, align_bytes=64, name=f"x_words_{s}") for s in range(passes)]
+        x_scales = [keep.tile([P, S], U8, align_bytes=64, name=f"x_scales_{s}") for s in range(passes)]
+        picked = [keep.tile([P, PACK, S], F32, name=f"picked_{s}") for s in range(passes)]
         w1_words, w1_scales, h_words, h_scales, w2_words, w2_scales = {}, {}, {}, {}, {}, {}
 
         def cast(eng, out, in_):
@@ -80,23 +88,21 @@ def tile_picked_sub_mlp_relu_sub_e_kernel(tc, xT, w1, w2, gate, offs, pos1, pos2
             else:
                 nc.scalar.activation(out=out, in_=in_, func=COPY)
 
-        def x_stage(s, c, parts):
-            grp = keep.tile([P, X_COLS, PACK], BF16, align_bytes=64, name=f"x_grp_{s}_{c}")
+        def x_gather(s, j):
+            nc.vector.tensor_copy(out=picked[s][:, j, :], in_=x_raw[s, j][:].indirect(offs_t[:]))
+
+        def x_stage(s, parts, width):
+            grp = keep.tile([P, S, PACK], BF16, align_bytes=64, name=f"x_grp_{s}")
             for a, b, eng in parts:
                 dst = grp[:, a:b, :].rearrange("p (c i) j -> p c j i", i=4)
-                src = x_raw[s][:, :, c * X_COLS + a : c * X_COLS + b].rearrange("p j (c i) -> p c j i", i=4)
+                src = picked[s][:, :, a:b].rearrange("p j (c i) -> p c j i", i=4)
                 cast(eng, dst, src)
-            nc.vector.quantize_mx(
-                out=x_words[s][:, c * X_COLS : (c + 1) * X_COLS].bitcast(FP8X4),
-                scales=x_scales[4 * s : P, c * X_COLS : (c + 1) * X_COLS],
-                in_=grp[:].rearrange("p c j -> p (c j)"),
-            )
-
-        def x_gather(s):
-            nc.vector.tensor_copy(out=xg_words[s][:], in_=x_words[s][:].indirect(offs_t[:]))
-
-        def x_gather_scales():
-            nc.vector.tensor_copy(out=xg_scales[:], in_=x_scales[:].indirect(offs_t[:]))
+            for a in range(0, S, width):
+                nc.vector.quantize_mx(
+                    out=x_words[s][:, a : a + width].bitcast(FP8X4),
+                    scales=x_scales[s][:, a : a + width],
+                    in_=grp[:, a : a + width, :].rearrange("p c j -> p (c j)"),
+                )
 
         def w1_stage(h, s, parts, t_quant):
             grp = keep.tile([P, PACK, P, PACK], BF16, align_bytes=64, name=f"w1_grp_{h}_{s}")
@@ -120,15 +126,15 @@ def tile_picked_sub_mlp_relu_sub_e_kernel(tc, xT, w1, w2, gate, offs, pos1, pos2
             hg = keep.tile([P, S, PACK], BF16, align_bytes=64, name=f"h_grp_{h}")
             for q in range(S // QUARTER):
                 cols = slice(q * QUARTER, (q + 1) * QUARTER)
-                bank = psum_h.tile([P, PACK, QUARTER], F32, name="h_bank")
+                bank = psum.tile([P, PACK, QUARTER], F32, name=f"h_bank_{h}_{q}", tag=f"bank_{h}_{q}")
                 for t in range(PACK):
                     for s in range(passes):
                         nc.tensor.matmul_mx(
                             out=bank[:, t, :],
                             lhsT=w1_words[h, s][:, t * P : (t + 1) * P].bitcast(FP8X4),
                             lhsT_scale=w1_scales[h, s][:, t * P : (t + 1) * P],
-                            rhs=xg_words[s][:, cols].bitcast(FP8X4),
-                            rhs_scale=xg_scales[4 * s : P, cols],
+                            rhs=x_words[s][:, cols].bitcast(FP8X4),
+                            rhs_scale=x_scales[s][:, cols],
                             start=(s == 0),
                             stop=(s == passes - 1),
                         )
@@ -157,25 +163,28 @@ def tile_picked_sub_mlp_relu_sub_e_kernel(tc, xT, w1, w2, gate, offs, pos1, pos2
                 out=w2_words[s][:].bitcast(FP8X4), scales=w2_scales[s][:], in_=grp[:].rearrange("p c j -> p (c j)")
             )
 
-        x_stage(0, 0, ((0, 192, "v"), (192, 512, "s"),))
-        x_stage(0, 1, ((0, 320, "v"), (320, 512, "s"),))
-        x_stage(1, 0, ((0, 256, "v"), (256, 512, "s"),))
-        x_stage(1, 1, ((0, 192, "v"), (192, 512, "s"),))
-        x_gather(0)
-        x_gather(1)
-        x_gather_scales()
-        w1_stage(0, 0, ((0, 40, "v"), (40, 128, "s"),), 4)
-        w1_stage(0, 1, ((0, 40, "v"), (40, 128, "s"),), 4)
-        w1_stage(1, 0, ((0, 40, "v"), (40, 128, "s"),), 4)
-        w1_stage(1, 1, ((0, 80, "v"), (80, 128, "s"),), 4)
-        h_stage(0, "ssss", 2)
-        w2_stage(0, ((0, 128, "v"), (128, 256, "s"),))
-        w2_stage(1, ((0, 128, "v"), (128, 256, "s"),))
-        h_stage(1, "svss", 1)
+        w1_stage(0, 0, ((0, 24, "v"), (24, 128, "s"),), 4)
+        x_gather(0, 0)
+        x_gather(0, 1)
+        x_gather(0, 2)
+        x_gather(0, 3)
+        x_stage(0, ((0, 512, "s"),), 512)
+        x_gather(1, 0)
+        x_gather(1, 1)
+        x_gather(1, 2)
+        x_gather(1, 3)
+        x_stage(1, ((0, 320, "v"), (320, 512, "s"),), 512)
+        w1_stage(0, 1, ((0, 56, "v"), (56, 128, "s"),), 4)
+        w1_stage(1, 0, ((0, 72, "v"), (72, 128, "s"),), 4)
+        w1_stage(1, 1, ((0, 56, "v"), (56, 64, "s"), (64, 120, "v"), (120, 128, "s"),), 1)
+        h_stage(0, "ssss", 4)
+        w2_stage(0, ((0, 64, "v"), (64, 256, "s"),))
+        w2_stage(1, ((0, 256, "v"),))
+        h_stage(1, "sssv", 1)
 
-        y_bank = [psum_y.tile([P, S], F32, name=f"y_bank_{m}") for m in range(N // P)]
+        y_bank = [psum.tile([P, S], F32, name=f"y_bank_{m}", tag=f"bank_0_{m}") for m in range(N // P)]
         y = [keep.tile([P, S], F32, name=f"y_{m}") for m in range(N // P)]
-        for n0, n1 in ((0, 256), (256, 384), (384, 512)):
+        for n0, n1 in ((0, 256), (256, 512)):
             cols = slice(n0, n1)
             for m in range(N // P):
                 m_cols = slice(m * P, (m + 1) * P)

@@ -107,8 +107,8 @@ def tile_picked_sub_mlp_relu_sub_e_kernel(tc, xT, w1, w2, gate, offs, pos1, pos2
         def w1_stage(h, s, parts, t_quant):
             grp = keep.tile([P, PACK, P, PACK], BF16, align_bytes=64, name=f"w1_grp_{h}_{s}")
             for a, b, eng in parts:
-                dst = grp[:, :, a:b, :].rearrange("p t m j -> p m t j")
-                src = w1_raw[h, s][:, :, PACK * a : PACK * b].rearrange("p j (m t) -> p m t j", t=PACK)
+                dst = grp[:, :, a:b, :].rearrange("p t m j -> p m j t")
+                src = w1_raw[h, s][:, :, PACK * a : PACK * b].rearrange("p j (m t) -> p m j t", t=PACK)
                 cast(eng, dst, src)
             w1_words[h, s] = keep.tile([P, PASS], U32, align_bytes=64, name=f"w1_words_{h}_{s}")
             w1_scales[h, s] = keep.tile([P, PASS], U8, align_bytes=64, name=f"w1_scales_{h}_{s}")
@@ -200,12 +200,26 @@ def tile_picked_sub_mlp_relu_sub_e_kernel(tc, xT, w1, w2, gate, offs, pos1, pos2
                     )
                 nc.scalar.activation(out=y[m][:, cols], in_=y_bank[m][:, cols], func=COPY)
 
-        for m in range(N // P):
-            prod = keep.tile([P, D, V], F32, name=f"prod_{m}")
-            for d in range(D):
-                nc.vector.tensor_tensor(prod[:, d, :], y[m][:].indirect(pos_t[d][:]), gate_t[m][:, d, :], MULT)
-            pair = keep.tile([P, 2, V], F32, name=f"pair_{m}")
-            nc.vector.tensor_add(pair[:], prod[:, 0:2, :], prod[:, 2:4, :])
-            total = keep.tile([P, V], F32, name=f"total_{m}")
-            nc.vector.tensor_add(total[:], pair[:, 0, :], pair[:, 1, :])
-            nc.sync.dma_start(out=out[m * P : (m + 1) * P, :], in_=total[:])
+        prod = [keep.tile([P, D, V], F32, name=f"prod_{m}") for m in range(N // P)]
+
+        def y_gather(m, d):
+            nc.vector.tensor_tensor(prod[m][:, d, :], y[m][:].indirect(pos_t[d][:]), gate_t[m][:, d, :], MULT)
+
+        def add(name, in0, in1):
+            result = keep.tile([P, in0.shape[1], V] if len(in0.shape) == 3 else [P, V], F32, name=name)
+            nc.vector.tensor_add(result[:], in0, in1)
+            return result
+
+        for d in range(D):
+            y_gather(0, d)
+        y_gather(1, 0)
+        pair = add("pair", prod[0][:, 0:2, :], prod[0][:, 2:4, :])
+        y_gather(1, 1)
+        out_0 = add("out_0", pair[:, 0, :], pair[:, 1, :])
+        nc.sync.dma_start(out=out[0:P, :], in_=out_0[:])
+        y_gather(1, 2)
+        sum_01 = add("sum_01", prod[1][:, 0, :], prod[1][:, 1, :])
+        y_gather(1, 3)
+        sum_012 = add("sum_012", sum_01[:], prod[1][:, 2, :])
+        out_1 = add("out_1", sum_012[:], prod[1][:, 3, :])
+        nc.sync.dma_start(out=out[P : 2 * P, :], in_=out_1[:])

from contextlib import ExitStack

import concourse.mybir as mybir

K, T, D, S, V, H, N = 1024, 1024, 4, 512, 256, 1024, 256
FLOPS = 2 * S * (K * H + H * N) + 2 * D * N * V

F32 = mybir.dt.float32
BF16 = mybir.dt.bfloat16
U32 = mybir.dt.uint32
U16 = mybir.dt.uint16
U8 = mybir.dt.uint8
FP8X4 = mybir.dt.float8_e4m3fn_x4
MULT = mybir.AluOpType.mult
COPY = mybir.ActivationFunctionType.Copy
RELU = mybir.ActivationFunctionType.Relu

P = 128
PACK = 4
PASS = P * PACK
QUARTER = 128


def tile_picked_sub_mlp_relu_sub_e_kernel(tc, xT, w1, w2, gate, offs, pos1, pos2, pos3, pos4, out):
    nc = tc.nc
    passes = K // PASS
    halves = H // PASS

    with ExitStack() as ctx:
        lists = ctx.enter_context(tc.tile_pool(name="lists", bufs=1))
        keep = ctx.enter_context(tc.tile_pool(name="keep", bufs=1))
        psum = ctx.enter_context(tc.psum_pool(name="psum", bufs=1))

        warm = keep.tile([P, 1], F32, name="warm")
        nc.vector.memset(warm[:], 0.0)
        warm_out = keep.tile([P, 1], F32, name="warm_out")
        nc.scalar.activation(out=warm_out[:], in_=warm[:], func=RELU)

        offs_t = lists.tile([P, S // 16], U16, name="offs_t")
        nc.sync.dma_start(offs_t[:], offs)
        x_raw, w1_raw = {}, {}

        def load_x(s, j):
            x_raw[s, j] = keep.tile([P, T], F32, name=f"x_raw_{s}_{j}")
            view = xT[s * PASS : (s + 1) * PASS, :].rearrange("(p j) w -> p j w", j=PACK)
            nc.sync.dma_start(out=x_raw[s, j][:], in_=view[:, j, :])

        def load_w1(h, s, cuts):
            w1_raw[h, s] = keep.tile([P, PACK, PASS], F32, name=f"w1_raw_{h}_{s}")
            view = w1[s * PASS : (s + 1) * PASS, h * PASS : (h + 1) * PASS].rearrange("(p j) w -> p j w", j=PACK)
            for a, b in zip(cuts[:-1], cuts[1:]):
                nc.sync.dma_start(out=w1_raw[h, s][:, :, a:b], in_=view[:, :, a:b])

        load_x(0, 0)
        load_x(0, 1)
        load_x(0, 2)
        load_x(0, 3)
        load_x(1, 0)
        load_x(1, 1)
        load_x(1, 2)
        load_w1(0, 0, (0, PASS))
        load_x(1, 3)
        load_w1(0, 1, (0, PASS))
        load_w1(1, 0, (0, PASS))
        load_w1(1, 1, (0, PASS // 2, PASS))
        w2_raw = {}
        for s in range(halves):
            w2_raw[s] = keep.tile([P, PACK, N], F32, name=f"w2_raw_{s}")
            nc.sync.dma_start(
                out=w2_raw[s][:].rearrange("p j w -> p (j w)"),
                in_=w2[s * PASS : (s + 1) * PASS, :].rearrange("(p j) w -> p (j w)", j=PACK),
            )
        gate_t = [keep.tile([P, D, V], F32, name=f"gate_{m}") for m in range(N // P)]
        pos_t = [lists.tile([P, V // 16], U16, name=f"pos_{d}") for d in range(D)]
        nc.sync.dma_start(out=gate_t[0][:], in_=gate[:, 0:P, :].rearrange("d p v -> p d v"))
        for p_t, pos in zip(pos_t, (pos1, pos2, pos3, pos4)):
            nc.sync.dma_start(p_t[:], pos)
        nc.sync.dma_start(out=gate_t[1][:], in_=gate[:, P : 2 * P, :].rearrange("d p v -> p d v"))

        x_words = [keep.tile([P, S], U32, align_bytes=64, name=f"x_words_{s}") for s in range(passes)]
        x_scales = [keep.tile([P, S], U8, align_bytes=64, name=f"x_scales_{s}") for s in range(passes)]
        picked = [keep.tile([P, PACK, S], F32, name=f"picked_{s}") for s in range(passes)]
        w1_words, w1_scales, h_words, h_scales, w2_words, w2_scales = {}, {}, {}, {}, {}, {}

        def cast(eng, out, in_):
            if eng == "v":
                nc.vector.tensor_copy(out=out, in_=in_)
            else:
                nc.scalar.activation(out=out, in_=in_, func=COPY)

        def x_gather(s, j):
            nc.vector.tensor_copy(out=picked[s][:, j, :], in_=x_raw[s, j][:].indirect(offs_t[:]))

        def x_stage(s, parts, width):
            grp = keep.tile([P, S, PACK], BF16, align_bytes=64, name=f"x_grp_{s}")
            for a, b, eng in parts:
                dst = grp[:, a:b, :].rearrange("p (c i) j -> p c j i", i=4)
                src = picked[s][:, :, a:b].rearrange("p j (c i) -> p c j i", i=4)
                cast(eng, dst, src)
            for a in range(0, S, width):
                nc.vector.quantize_mx(
                    out=x_words[s][:, a : a + width].bitcast(FP8X4),
                    scales=x_scales[s][:, a : a + width],
                    in_=grp[:, a : a + width, :].rearrange("p c j -> p (c j)"),
                )

        def w1_stage(h, s, parts, t_quant):
            grp = keep.tile([P, PACK, P, PACK], BF16, align_bytes=64, name=f"w1_grp_{h}_{s}")
            for a, b, eng in parts:
                dst = grp[:, :, a:b, :].rearrange("p t m j -> p m j t")
                src = w1_raw[h, s][:, :, PACK * a : PACK * b].rearrange("p j (m t) -> p m j t", t=PACK)
                cast(eng, dst, src)
            w1_words[h, s] = keep.tile([P, PASS], U32, align_bytes=64, name=f"w1_words_{h}_{s}")
            w1_scales[h, s] = keep.tile([P, PASS], U8, align_bytes=64, name=f"w1_scales_{h}_{s}")
            for t in range(0, PACK, t_quant):
                cols = slice(t * P, (t + t_quant) * P)
                nc.vector.quantize_mx(
                    out=w1_words[h, s][:, cols].bitcast(FP8X4),
                    scales=w1_scales[h, s][:, cols],
                    in_=grp[:, t : t + t_quant, :, :].rearrange("p t m j -> p (t m j)"),
                )

        def h_stage(h, engines, q_quant):
            h_words[h] = keep.tile([P, S], U32, align_bytes=64, name=f"h_words_{h}")
            h_scales[h] = keep.tile([P, S], U8, align_bytes=64, name=f"h_scales_{h}")
            hg = keep.tile([P, S, PACK], BF16, align_bytes=64, name=f"h_grp_{h}")
            for q in range(S // QUARTER):
                cols = slice(q * QUARTER, (q + 1) * QUARTER)
                bank = psum.tile([P, PACK, QUARTER], F32, name=f"h_bank_{h}_{q}", tag=f"bank_{h}_{q}")
                for t in range(PACK):
                    for s in range(passes):
                        nc.tensor.matmul_mx(
                            out=bank[:, t, :],
                            lhsT=w1_words[h, s][:, t * P : (t + 1) * P].bitcast(FP8X4),
                            lhsT_scale=w1_scales[h, s][:, t * P : (t + 1) * P],
                            rhs=x_words[s][:, cols].bitcast(FP8X4),
                            rhs_scale=x_scales[s][:, cols],
                            start=(s == 0),
                            stop=(s == passes - 1),
                        )
                src = bank[:].rearrange("p t n -> p n t")
                if engines[q] == "v":
                    nc.vector.tensor_scalar_max(out=hg[:, cols, :], in0=src, scalar1=0.0)
                else:
                    nc.scalar.activation(out=hg[:, cols, :], in_=src, func=RELU)
                if (q + 1) % q_quant == 0:
                    cols = slice((q + 1 - q_quant) * QUARTER, (q + 1) * QUARTER)
                    nc.vector.quantize_mx(
                        out=h_words[h][:, cols].bitcast(FP8X4),
                        scales=h_scales[h][:, cols],
                        in_=hg[:, cols, :].rearrange("p n t -> p (n t)"),
                    )

        def w2_stage(s, parts):
            grp = keep.tile([P, N, PACK], BF16, align_bytes=64, name=f"w2_grp_{s}")
            for a, b, eng in parts:
                dst = grp[:, a:b, :].rearrange("p (c i) j -> p c j i", i=4)
                src = w2_raw[s][:, :, a:b].rearrange("p j (c i) -> p c j i", i=4)
                cast(eng, dst, src)
            w2_words[s] = keep.tile([P, N], U32, align_bytes=64, name=f"w2_words_{s}")
            w2_scales[s] = keep.tile([P, N], U8, align_bytes=64, name=f"w2_scales_{s}")
            nc.vector.quantize_mx(
                out=w2_words[s][:].bitcast(FP8X4), scales=w2_scales[s][:], in_=grp[:].rearrange("p c j -> p (c j)")
            )

        w1_stage(0, 0, ((0, 24, "v"), (24, 128, "s"),), 4)
        x_gather(0, 0)
        x_gather(0, 1)
        x_gather(0, 2)
        x_gather(0, 3)
        x_stage(0, ((0, 512, "s"),), 512)
        x_gather(1, 0)
        x_gather(1, 1)
        x_gather(1, 2)
        x_gather(1, 3)
        x_stage(1, ((0, 320, "v"), (320, 512, "s"),), 512)
        w1_stage(0, 1, ((0, 56, "v"), (56, 128, "s"),), 4)
        w1_stage(1, 0, ((0, 72, "v"), (72, 128, "s"),), 4)
        w1_stage(1, 1, ((0, 56, "v"), (56, 64, "s"), (64, 120, "v"), (120, 128, "s"),), 1)
        h_stage(0, "ssss", 4)
        w2_stage(0, ((0, 64, "v"), (64, 256, "s"),))
        w2_stage(1, ((0, 256, "v"),))
        h_stage(1, "sssv", 1)

        y_bank = [psum.tile([P, S], F32, name=f"y_bank_{m}", tag=f"bank_0_{m}") for m in range(N // P)]
        y = [keep.tile([P, S], F32, name=f"y_{m}") for m in range(N // P)]
        for n0, n1 in ((0, 256), (256, 512)):
            cols = slice(n0, n1)
            for m in range(N // P):
                m_cols = slice(m * P, (m + 1) * P)
                for s in range(halves):
                    nc.tensor.matmul_mx(
                        out=y_bank[m][:, cols],
                        lhsT=w2_words[s][:, m_cols].bitcast(FP8X4),
                        lhsT_scale=w2_scales[s][:, m_cols],
                        rhs=h_words[s][:, cols].bitcast(FP8X4),
                        rhs_scale=h_scales[s][:, cols],
                        start=(s == 0),
                        stop=(s == halves - 1),
                    )
                nc.scalar.activation(out=y[m][:, cols], in_=y_bank[m][:, cols], func=COPY)

        prod = [keep.tile([P, D, V], F32, name=f"prod_{m}") for m in range(N // P)]

        def y_gather(m, d):
            nc.vector.tensor_tensor(prod[m][:, d, :], y[m][:].indirect(pos_t[d][:]), gate_t[m][:, d, :], MULT)

        def add(name, in0, in1):
            result = keep.tile([P, in0.shape[1], V] if len(in0.shape) == 3 else [P, V], F32, name=name)
            nc.vector.tensor_add(result[:], in0, in1)
            return result

        for d in range(D):
            y_gather(0, d)
        y_gather(1, 0)
        pair = add("pair", prod[0][:, 0:2, :], prod[0][:, 2:4, :])
        y_gather(1, 1)
        out_0 = add("out_0", pair[:, 0, :], pair[:, 1, :])
        nc.sync.dma_start(out=out[0:P, :], in_=out_0[:])
        y_gather(1, 2)
        sum_01 = add("sum_01", prod[1][:, 0, :], prod[1][:, 1, :])
        y_gather(1, 3)
        sum_012 = add("sum_012", sum_01[:], prod[1][:, 2, :])
        out_1 = add("out_1", sum_012[:], prod[1][:, 3, :])
        nc.sync.dma_start(out=out[P : 2 * P, :], in_=out_1[:])
